import numpy as np, ml_dtypes
CORES = [5,29,101,125,133,157,229,253]
N = 8
import mx_ref
NC, KT, G, WT = 128, 1, 4, 2
C = np.float32(0.043)
BF = ml_dtypes.bfloat16
def cut(t, i, w=512):
    return t[:, w * i:w * i + w]
def tile(rs):
    return np.stack(rs, axis=2).reshape(128, -1).astype(BF)
def layer(w, X):
    out = []
    for i in range(G):
        for t in range(len(X)):
            p = mx_ref.matmul(mx_ref.quantize(cut(w, len(X) * i + t)), X[t])
            z = p if t == 0 else z + p
        out.append(z)
    return out
def act(Z):
    return [np.maximum(z, 0) * C for z in Z]
def setup_inputs(rng):
    def f(*shape):
        return mx_ref.flush((rng.standard_normal(shape, dtype=np.float32) * np.exp2(rng.integers(-2, 3, shape[:-1] + (1,)))).astype(BF))
    return {"x": f(N, 128, KT * 4 * NC), "w1": f(N, 128, G * KT * 512), "w2": f(N, 128, WT * 512)}
def setup_inputs_blocks(rng):
    d = setup_inputs(rng)
    for k in ("x", "w1", "w2"): d[k] = mx_ref.spread(d[k], rng, 4)
    return d
def setup_inputs_wide(rng):
    d = setup_inputs(rng)
    for k in ("x", "w1", "w2"): d[k] = mx_ref.flush((d[k].astype(np.float32) * np.exp2(rng.integers(-8, 9, (N, 1, 1))).astype(np.float32)).astype(BF))
    return d
def setup_inputs_zeros(rng):
    d = setup_inputs(rng); v = d["x"].reshape(N, 128, -1, 4).copy()
    v[np.broadcast_to((rng.random((N, 1, v.shape[2], 1)) < 0.33), v.shape)] = 0
    d["x"] = v.reshape(d["x"].shape)
    return d
def reference(x, w1, w2):
    H = [mx_ref.quantize(tile(act(layer(w1[j], [mx_ref.quantize(cut(x[j], t, 4 * NC)) for t in range(KT)])))) for j in range(N)]
    y = np.zeros((N, 128, N * WT * NC), np.float32)
    for r in range(N):
        for i in range(WT):
            qw = mx_ref.quantize(cut(w2[r], i))
            for j in range(N):
                y[r][:, NC * (WT * j + i):NC * (WT * j + i) + NC] = mx_ref.matmul(qw, H[j])
    return {"y": y}

from concourse.bass import DstId, RemoteDMATransfer
from concourse.mybir import dt, AluOpType, ActivationFunctionType

N = 8
NC = 128
G = 4
WT = 2
C = 0.043
BANK = 512
BANKS = 8

SCRATCH = {
    "xb": ("sbuf", [128, 4 * NC], "bfloat16"),
    "w1b": ("sbuf", [128, G * 512], "bfloat16"),
    "w2b": ("sbuf", [128, WT * 512], "bfloat16"),
    "hb": ("sbuf", [128, 4 * NC], "bfloat16"),
    "xq": ("sbuf", [128, NC], "float8_e4m3fn_x4"),
    "xs": ("sbuf", [128, NC], "uint8"),
    "w1q": ("sbuf", [128, G * 128], "float8_e4m3fn_x4"),
    "w1s": ("sbuf", [128, G * 128], "uint8"),
    "w2q": ("sbuf", [128, WT * 128], "float8_e4m3fn_x4"),
    "w2s": ("sbuf", [128, WT * 128], "uint8"),
    "hq": ("sbuf", [128, N * NC], "float8_e4m3fn_x4"),
    "hs": ("sbuf", [128, N * NC], "uint8"),
    "ps": ("psum", [128, BANKS * BANK], "float32"),
    "yb": ("sbuf", [128, N * WT * NC], "float32"),
}
SEMAPHORES = (["ldx", "ldw1", "ldw2", "qx", "ac", "qh", "qw2", "st", "sent", "issued"]
              + ["qa%d" % i for i in range(G)] + ["ma%d" % i for i in range(G)]
              + ["a%d" % j for j in range(N)]
              + ["m%d_%d" % (i, t) for i in range(WT) for t in range(N)]
              + ["cp%d" % t for t in range(N)])


def _count(mask):
    return bin(mask).count("1")


def _plan(R, cores, topo):
    mine = [c for c in cores if c == R or topo.same_plane(R, c)]
    far = [c for c in cores if c not in mine]
    k = mine.index(R)
    direct = [mine[(k + s) % len(mine)] for s in range(1, len(mine))]
    cross = [far[(k + s) % len(far)] for s in range(len(far))]
    w = topo.CORES_PER_CHIP
    chipmates = [c for c in range(max(R - w + 1, 0), R + w)
                 if c != R and topo.host(c) == topo.host(R) and topo.chip(c) == topo.chip(R)]
    ports = [c for c in chipmates if all(topo.may_write(c, d) for d in cross)]
    near = [c for c in ports if topo.die(c) == topo.die(R)]
    away = [c for c in ports if topo.die(c) != topo.die(R)]
    half = len(cross) // 2
    relays = {"c": [(near[0], cross[:half]), (away[0], cross[half:])],
              "p": [(away[1], cross[:half]), (near[1], cross[half:])]}
    order = ([R] + [mine[(k - s) % len(mine)] for s in range(1, len(mine))]
             + [far[(k - s) % len(far)] for s in (0, 2, 1, 3)])
    return direct, relays, order


def _view(T, kind, j):
    if kind == "c":
        return T.hq[:, NC * j:NC * j + NC].bitcast(dt.uint8)
    return T.hs[:, NC * j:NC * j + NC]


def _transfer(T, topo, src, dests, mask, kind, j):
    ids = []
    for d in dests:
        rid, pid = topo.addr(d, src)
        ids.append(DstId(rid=rid, pnc=pid))
    return RemoteDMATransfer(dst_ids=ids, dma_engine_mask=mask, remote_sem=T.sem["a%d" % j],
                             srcs=[_view(T, kind, j)], dsts=[_view(T, kind, j) for _ in dests])


def _relay(g, core, T, topo):
    for R in T.cores:
        j = T.rank_of(R)
        direct, relays, _ = _plan(R, T.cores, topo)
        for kind in ("c", "p"):
            for h, dests in relays[kind]:
                if h != core:
                    continue
                fed = _count(topo.mask(R, h) & ~topo.mask(R, direct[0]))
                mask = topo.mask(core, dests[0])
                g.wait_ge(T.sem["a%d" % j], fed)
                g.remote_dma_fused([_transfer(T, topo, core, dests, mask, kind, j)], local_sem=T.sem.sent)
                g.wait_ge(T.sem.sent, _count(mask))


def rank_program(g, core, T, topo):
    rank = T.rank_of(core)
    if rank is None:
        _relay(g, core, T, topo)
        return
    direct, relays, order = _plan(core, T.cores, topo)
    sem = T.sem
    ve, sc, te, sy = g.vector, g.scalar, g.tensor, g.sync

    def bank(b):
        return T.ps[:, BANK * b:BANK * b + NC]

    def bank2(t, i):
        return bank((G + WT * t + i) % BANKS)

    own_q, own_s = T.hq[:, NC * rank:NC * rank + NC], T.hs[:, NC * rank:NC * rank + NC]

    sy.dma_start(T.xb[:], T.x[:]).then_inc(sem.ldx, 16)
    sc.dma_start(T.w1b[:], T.w1[:]).then_inc(sem.ldw1, 16)
    sy.dma_start(T.w2b[:], T.w2[:]).then_inc(sem.ldw2, 16)

    ve.wait_ge(sem.ldx, 16)
    ve.quantize_mx(T.xq[:], T.xs[:], T.xb[:]).then_inc(sem.qx, 1)
    ve.wait_ge(sem.ldw1, 16)
    for i in range(G):
        ve.quantize_mx(T.w1q[:, 128 * i:128 * i + 128], T.w1s[:, 128 * i:128 * i + 128],
                       T.w1b[:, 512 * i:512 * i + 512]).then_inc(sem["qa%d" % i], 1)
    ve.wait_ge(sem["ma%d" % (G - 1)], 1)
    ve.tensor_scalar(T.hb[:, G - 1:4 * NC:4], bank(G - 1), 0.0, C, AluOpType.max, AluOpType.mult).then_inc(sem.ac, 1)
    ve.wait_ge(sem.ac, G)
    ve.quantize_mx(own_q, own_s, T.hb[:]).then_inc(sem.qh, 1)
    ve.wait_ge(sem.ldw2, 16)
    ve.quantize_mx(T.w2q[:], T.w2s[:], T.w2b[:]).then_inc(sem.qw2, 1)

    for b in range(G - 1):
        sc.wait_ge(sem["ma%d" % b], 1)
        sc.activation(T.hb[:, b:4 * NC:4], bank(b), ActivationFunctionType.Relu, scale=C).then_inc(sem.ac, 1)

    te.wait_ge(sem.qx, 1)
    for i in range(G):
        te.wait_ge(sem["qa%d" % i], 1)
        te.matmul_mx(bank(i), T.w1q[:, 128 * i:128 * i + 128], T.w1s[:, 128 * i:128 * i + 128],
                     T.xq[:], T.xs[:], True, True).then_inc(sem["ma%d" % i], 1)

    off = topo.mask(core, direct[0])
    chip_only = topo.mask(core, relays["c"][0][0]) & ~off
    g.wait_ge(sem.qh, 1)
    for kind in ("c", "p"):
        g.remote_dma_fused([
            _transfer(T, topo, core, [h for h, _ in relays[kind]], chip_only, kind, rank),
            _transfer(T, topo, core, direct, off, kind, rank),
        ], local_sem=sem.sent)
    g.sem_inc(sem.issued, 1)
    g.wait_ge(sem.sent, 2 * (_count(off) + _count(chip_only)))

    te.wait_ge(sem.qw2, 1)
    for t, src in enumerate(order):
        j = T.rank_of(src)
        if t == 0:
            te.wait_ge(sem.qh, 1)
            te.wait_ge(sem.ac, G)
        elif src in direct:
            te.wait_ge(sem["a%d" % j], 2 * _count(topo.mask(src, core)))
        else:
            te.wait_ge(sem["a%d" % j], sum(_count(topo.mask(h, core))
                                           for kind in ("c", "p") for h, ds in _plan(src, T.cores, topo)[1][kind] if core in ds))
        if t >= BANKS // WT:
            te.wait_ge(sem["cp%d" % (t - BANKS // WT)], WT)
        for i in range(WT):
            te.matmul_mx(bank2(t, i), T.w2q[:, 128 * i:128 * i + 128], T.w2s[:, 128 * i:128 * i + 128],
                         T.hq[:, NC * j:NC * j + NC], T.hs[:, NC * j:NC * j + NC], True, True).then_inc(sem["m%d_%d" % (i, t)], 1)
        lo = WT * NC * j
        ve.wait_ge(sem["m0_%d" % t], 1)
        ve.tensor_copy(T.yb[:, lo:lo + NC], bank2(t, 0)).then_inc(sem["cp%d" % t], 1)
        sc.wait_ge(sem["m1_%d" % t], 1)
        sc.activation(T.yb[:, lo + NC:lo + 2 * NC], bank2(t, 1), ActivationFunctionType.Copy).then_inc(sem["cp%d" % t], 1)
        if t == 0:
            sy.wait_ge(sem.issued, 1)
        sy.wait_ge(sem["cp%d" % t], WT)
        sy.dma_start(T.y[:, lo:lo + WT * NC], T.yb[:, lo:lo + WT * NC]).then_inc(sem.st, 16)
    sy.wait_ge(sem.st, 16 * N)
